import numpy as np
import ml_dtypes


def mxq(x, axis, fmt="e4m3"):
    dtype, down = {"e4m3": (ml_dtypes.float8_e4m3fn, 7), "e5m2": (ml_dtypes.float8_e5m2, 14)}[fmt]
    v = np.moveaxis(np.asarray(x, np.float32).astype(ml_dtypes.bfloat16).astype(np.float64), axis, -1)
    blocks = v.reshape(v.shape[:-1] + (-1, 32))
    amax = np.abs(blocks).max(-1, keepdims=True)
    byte = np.maximum(np.where(amax > 0, np.frexp(amax)[1] - 1 + 127, 0) - down, 1)
    scale = np.exp2(byte - 127.0)
    codes = (blocks / scale).astype(np.float32).astype(dtype).astype(np.float64)
    return np.moveaxis((codes * scale).reshape(v.shape), -1, axis)


WIDE = False


def mx_kscale(k):
    if not WIDE:
        return np.ones(k)
    levels = np.array([10, -10, 5, -5, 0])
    if k % 512:
        return np.exp2(np.random.permutation(np.resize(levels, k // 32))).repeat(32)
    a = np.empty((k // 512, 16))
    for p in range(k // 512):
        a[p, :8] = np.random.permutation(np.resize(levels, 8))
        for g in range(8):
            far = levels[np.abs(levels - a[p, g]) >= 10]
            a[p, g + 8] = far[np.random.randint(len(far))]
    return np.exp2(a.ravel()).repeat(32)


def f64(x):
    return np.asarray(x).astype(np.float64)


def striped(idx):
    return np.tile(np.asarray(idx).reshape(-1, 16).T, (8, 1)).astype(np.uint16)


def unstriped(offs):
    return offs[:16].T.reshape(-1).astype(np.int64)


E2M1 = np.array([0.0, 0.5, 1.0, 1.5, 2.0, 3.0, 4.0, 6.0, -0.0, -0.5, -1.0, -1.5, -2.0, -3.0, -4.0, -6.0])


def pack_weight(w, fmt):
    k, n = w.shape
    w = f64(np.asarray(w, np.float32).astype(ml_dtypes.bfloat16)).reshape(k // 32, 32, n)
    amax = np.abs(w).max(1)
    if fmt == "e4m3":
        byte = np.frexp(amax)[1] - 1 + 127 - 7
    else:
        mant, ex = np.frexp(amax / 6.0)
        byte = np.where(mant > 0.5, ex, ex - 1) + 127
    byte = np.clip(np.where(amax > 0, byte, 1), 1, 254)
    scaled = (w * np.exp2(127.0 - byte)[:, None, :]).reshape(k, n).astype(np.float32)
    by_word = np.ascontiguousarray(scaled.reshape(k // 512, 128, 4, n).transpose(0, 1, 3, 2))
    if fmt == "e4m3":
        words = by_word.astype(ml_dtypes.float8_e4m3fn).view(np.uint8)
    else:
        c = by_word.astype(ml_dtypes.float4_e2m1fn).view(np.uint8) & 0xF
        words = (c[..., 0::2] | (c[..., 1::2] << 4)).reshape(k // 512, 128, 2 * n)
    return np.ascontiguousarray(words), np.ascontiguousarray(byte.astype(np.uint8).reshape(k // 512, 16, n))


def unpack_weight(words, scales, fmt):
    g, _, n = scales.shape
    words = np.ascontiguousarray(words).reshape(g, 128, n, -1)
    if fmt == "e4m3":
        vals = words.view(ml_dtypes.float8_e4m3fn).astype(np.float64)
    else:
        nib = np.empty((g, 128, n, 4), np.uint8)
        nib[..., 0::2] = words & 0xF
        nib[..., 1::2] = words >> 4
        vals = E2M1[nib]
    vals = vals * np.repeat(np.exp2(scales.astype(np.float64) - 127.0), 8, axis=1)[..., None]
    return vals.transpose(0, 1, 3, 2).reshape(g * 512, n)


K, R, F, T, J, G = 512, 128, 512, 2048, 512, 64


def setup_inputs():
    n = np.random.standard_normal
    idx = np.random.permutation(T)[:J]
    fk = mx_kscale(K)
    ff = mx_kscale(F)
    tabp = pack_weight(n((K, T)) / fk[:, None], "e4m3")
    dtabp = pack_weight(n((K, T)) / fk[:, None], "e4m3")
    return {
        "tab_words": tabp[0],
        "tab_scales": tabp[1],
        "w1": (n((K, R)) * 1.5 / np.sqrt(K) * fk[:, None]).astype(np.float32),
        "w2": (n((K, R)) * 0.7 / np.sqrt(K) * fk[:, None]).astype(np.float32),
        "wo": (n((F, R)) * 1 / np.sqrt(F) * ff[:, None]).astype(np.float32),
        "dy": (n((F, G)) / ff[:, None]).astype(np.float32),
        "dtab_words": dtabp[0],
        "dtab_scales": dtabp[1],
        "og": (np.random.uniform(0.7, 2.0, (R, 1))).astype(np.float32),
        "base": (0.3 * n((R, J))).astype(np.float32),
        "offs": striped(idx),
    }


def reference(tab_words, tab_scales, w1, w2, wo, dy, dtab_words, dtab_scales, og, base, offs):
    idx = unstriped(offs)
    tabu = unpack_weight(tab_words, tab_scales, "e4m3")
    dtabu = unpack_weight(dtab_words, dtab_scales, "e4m3")
    w1q = mxq(f64(w1), 0, "e4m3")
    tabidxg = tabu[:, idx]
    a = w1q.T @ tabidxg
    dtabidxg = dtabu[:, idx]
    ta = w1q.T @ dtabidxg
    w2q = mxq(f64(w2), 0, "e4m3")
    b = w2q.T @ tabidxg
    tb = w2q.T @ dtabidxg
    p = np.exp(b)
    z = p.reshape(R, G, J // G).sum(axis=2)
    n1 = (p * a).reshape(R, G, J // G).sum(axis=2)
    u1 = np.tanh(n1 / z)
    woq = mxq(f64(wo), 0, "e4m3")
    dyq = mxq(f64(dy), 0, "e4m3")
    c0 = woq.T @ dyq
    dn1 = c0 * (1.0 - np.square(u1)) / z
    r1 = np.repeat(dn1, J // G, axis=1)
    dz = c0 * (1.0 - np.square(u1)) * n1 / np.square(z) * (-1.0)
    r2 = np.repeat(dz, J // G, axis=1)
    dp = r1 * a + r2
    xp = tb * p
    xz = xp.reshape(R, G, J // G).sum(axis=2)
    xn1 = (xp * a + ta * p).reshape(R, G, J // G).sum(axis=2)
    xu1 = (xn1 - xz * n1 / z) / z * (1.0 - np.square(u1))
    xdn1 = (xu1 * u1 * 2.0 * (-1.0) * c0 - xz * c0 * (1.0 - np.square(u1)) / z) / z
    xr1 = np.repeat(xdn1, J // G, axis=1)
    xdz = (xu1 * u1 * 2.0 * (-1.0) * c0 * n1 + xn1 * c0 * (1.0 - np.square(u1)) - xz * z * 2.0 * c0 * (1.0 - np.square(u1)) * n1 / np.square(z)) / np.square(z) * (-1.0)
    xr2 = np.repeat(xdz, J // G, axis=1)
    xdp = xr1 * a + ta * r1 + xr2
    xdb = xdp * p + xp * dp
    y = xdb * f64(og) + f64(base)
    return y

@@ -1,0 +1,201 @@
+from contextlib import ExitStack
+
+import concourse.mybir as mybir
+
+K, R, F, T, J, G = 512, 128, 512, 2048, 512, 64
+FLOPS = 2 * K * R * J * 4 + 2 * F * R * G
+
+F32 = mybir.dt.float32
+BF16 = mybir.dt.bfloat16
+I32 = mybir.dt.int32
+U32 = mybir.dt.uint32
+U16 = mybir.dt.uint16
+U8 = mybir.dt.uint8
+FP8X4 = mybir.dt.float8_e4m3fn_x4
+ACT = mybir.ActivationFunctionType
+ALU = mybir.AluOpType
+AX = mybir.AxisListType
+
+P = 128
+PACK = 4
+POOL = J // G
+HALVES = 2
+JH = J // HALVES
+GH = G // HALVES
+
+
+def tile_attend_hvgatepool_kernel(tc, tab_words, tab_scales, w1, w2, wo, dy, dtab_words, dtab_scales, og, base, offs, out):
+    nc = tc.nc
+    with ExitStack() as ctx:
+        sb = ctx.enter_context(tc.tile_pool(name="sb", bufs=1))
+        ps = ctx.enter_context(tc.psum_pool(name="ps", bufs=1))
+
+        def load_words(words, name):
+            window = sb.tile([P, T], U32, name=name)
+            nc.sync.dma_start(out=window[:].bitcast(I32), in_=words[0].rearrange("p n t -> p (n t)").bitcast(I32))
+            return window
+
+        def zeroed_scale_window(name, engine):
+            window = sb.tile([P, T], U8, name=name)
+            engine.memset(window[:].bitcast(I32), 0)
+            return window
+
+        def load_scales(window, scales, queue):
+            for q in range(4):
+                queue.dma_start(out=window[32 * q : 32 * q + 4, :].bitcast(I32), in_=scales[0, 4 * q : 4 * q + 4, :].bitcast(I32))
+
+        def load_rows(rows, name):
+            raw = sb.tile([P, PACK, rows.shape[1]], F32, name=name)
+            nc.sync.dma_start(out=raw[:], in_=rows.rearrange("(p t) c -> p t c", t=PACK))
+            return raw
+
+        def interleave(grouped, raw):
+            nc.scalar.copy(
+                out=grouped.rearrange("p (c i t) -> p c t i", i=4, t=PACK),
+                in_=raw[:].rearrange("p t (c i) -> p c t i", i=4),
+            )
+
+        def quantize(grouped, name):
+            width = grouped.shape[1] // PACK
+            codes = sb.tile([P, width], U32, name=name + "_codes", align_bytes=64)
+            scales = sb.tile([P, width], U8, name=name + "_scales", align_bytes=64)
+            nc.vector.quantize_mx(out=codes[:].bitcast(FP8X4), scales=scales[:], in_=grouped)
+            return codes[:], scales[:]
+
+        def product(acc, lhs, rhs_codes, rhs_scales):
+            nc.tensor.matmul_mx(out=acc, lhsT=lhs[0].bitcast(FP8X4), lhsT_scale=lhs[1],
+                                rhs=rhs_codes.bitcast(FP8X4), rhs_scale=rhs_scales, start=True, stop=True)
+
+        def by_group(ap):
+            return ap.rearrange("p (g i) -> p g i", i=POOL)
+
+        def spread(ap):
+            return ap.unsqueeze(2).to_broadcast([P, ap.shape[1], POOL])
+
+        offsets = sb.tile([P, J // 16], U16, name="offsets")
+        nc.sync.dma_start(offsets[:], offs)
+        tab_scale_window = zeroed_scale_window("tab_scale_window", nc.vector)
+        dtab_scale_window = zeroed_scale_window("dtab_scale_window", nc.vector)
+        w2_raw = load_rows(w2, "w2_raw")
+        load_scales(tab_scale_window, tab_scales, nc.sync)
+        tab_window = load_words(tab_words, "tab_window")
+        w1_raw = load_rows(w1, "w1_raw")
+        load_scales(dtab_scale_window, dtab_scales, nc.sync)
+        wo_raw = load_rows(wo, "wo_raw")
+        dy_raw = load_rows(dy, "dy_raw")
+        dtab_window = load_words(dtab_words, "dtab_window")
+        gain = sb.tile([P, 1], F32, name="gain")
+        nc.sync.dma_start(out=gain[:], in_=og)
+        base_sb = sb.tile([P, J], F32, name="base_sb")
+        nc.sync.dma_start(out=base_sb[:], in_=base)
+
+        def cast_and_quantize(raw, name):
+            grouped = sb.tile([P, raw.shape[2] * PACK], BF16, name=name + "_bf", align_bytes=64)
+            interleave(grouped[:], raw)
+            return quantize(grouped[:], name)
+
+        tab_s = sb.tile([P, J], U8, name="tab_s", align_bytes=64)
+        nc.vector.tensor_copy(tab_s[:], tab_scale_window[:].indirect(offsets[:]))
+        w2_q = cast_and_quantize(w2_raw, "w2")
+
+        cols = [slice(h * JH, (h + 1) * JH) for h in range(HALVES)]
+        groups = [slice(h * GH, (h + 1) * GH) for h in range(HALVES)]
+        lists = [offsets[:, h * JH // 16 : (h + 1) * JH // 16] for h in range(HALVES)]
+
+        a_ps = [ps.tile([P, JH], F32, name="a_ps%d" % h) for h in range(HALVES)]
+        b_ps = [ps.tile([P, JH], F32, name="b_ps%d" % h) for h in range(HALVES)]
+        t_ps = [ps.tile([P, 2, JH], F32, name="t_ps%d" % h) for h in range(HALVES)]
+        c_ps = ps.tile([P, G], F32, name="c_ps")
+
+        p_pa = sb.tile([P, 2, J], F32, name="p_pa")
+        z_n = sb.tile([P, 2, G], F32, name="z_n")
+        coef = sb.tile([P, 2, G], F32, name="coef")
+        mean = sb.tile([P, G], F32, name="mean")
+        u = sb.tile([P, G], F32, name="u")
+        usq = sb.tile([P, G], F32, name="usq")
+        a0 = sb.tile([P, G], F32, name="a0")
+        an = sb.tile([P, G], F32, name="an")
+        dev = sb.tile([P, J], F32, name="dev")
+        sn = sb.tile([P, J], F32, name="sn")
+        w_a = sb.tile([P, J], F32, name="w_a")
+        w_b = sb.tile([P, J], F32, name="w_b")
+        wt = sb.tile([P, 2, J], F32, name="wt")
+        xs = sb.tile([P, 2, G], F32, name="xs")
+        xc = sb.tile([P, 2, G], F32, name="xc")
+        t2 = sb.tile([P, G], F32, name="t2")
+        cc = sb.tile([P, G], F32, name="cc")
+        e1 = sb.tile([P, J], F32, name="e1")
+        e2 = sb.tile([P, J], F32, name="e2")
+        e3 = sb.tile([P, J], F32, name="e3")
+        rest = sb.tile([P, J], F32, name="rest")
+        y = sb.tile([P, J], F32, name="y")
+        p = p_pa[:, 0, :]
+        rz = coef[:, 0, :]
+
+        def group_sums(sums, terms, h):
+            nc.vector.tensor_reduce(sums[:, :, groups[h]], terms[:, :, cols[h]].rearrange("p k (g i) -> p k g i", i=POOL), AX.X, ALU.add)
+
+        def gather_directions(h):
+            dtab_w = sb.tile([P, JH], U32, name="dtab_w%d" % h, align_bytes=64)
+            nc.vector.tensor_copy(dtab_w[:], dtab_window[:].indirect(lists[h]))
+            product(t_ps[h][:, 0, :], w2_q, dtab_w[:], dtab_s[:, cols[h]])
+            product(t_ps[h][:, 1, :], w1_q, dtab_w[:], dtab_s[:, cols[h]])
+
+        tab_w = [sb.tile([P, JH], U32, name="tab_w%d" % h, align_bytes=64) for h in range(HALVES)]
+        for h in range(HALVES):
+            nc.vector.tensor_copy(tab_w[h][:], tab_window[:].indirect(lists[h]))
+            product(b_ps[h][:], w2_q, tab_w[h][:], tab_s[:, cols[h]])
+        w1_q = cast_and_quantize(w1_raw, "w1")
+        for h in range(HALVES):
+            nc.scalar.activation(p[:, cols[h]], b_ps[h][:], ACT.Exp)
+            product(a_ps[h][:], w1_q, tab_w[h][:], tab_s[:, cols[h]])
+        dtab_s = sb.tile([P, J], U8, name="dtab_s", align_bytes=64)
+        nc.vector.tensor_copy(dtab_s[:], dtab_scale_window[:].indirect(offsets[:]))
+        for h in range(HALVES):
+            nc.vector.tensor_tensor(p_pa[:, 1, cols[h]], a_ps[h][:], p[:, cols[h]], ALU.mult)
+        for h in range(HALVES):
+            group_sums(z_n, p_pa, h)
+
+        wo_q = cast_and_quantize(wo_raw, "wo")
+        dy_q = cast_and_quantize(dy_raw, "dy")
+        product(c_ps[:], wo_q, dy_q[0], dy_q[1])
+
+        nc.vector.reciprocal(rz, z_n[:, 0, :])
+        gather_directions(0)
+        nc.vector.tensor_tensor(mean[:], z_n[:, 1, :], rz, ALU.mult)
+        nc.vector.scalar_tensor_tensor(a0[:], c_ps[:], gain[:], rz, ALU.mult, ALU.mult)
+        nc.scalar.activation(u[:], mean[:], ACT.Tanh)
+        nc.scalar.activation(usq[:], u[:], ACT.Square)
+        gather_directions(1)
+        nc.vector.scalar_tensor_tensor(an[:], usq[:], -1.0, a0[:], ALU.add, ALU.mult)
+        nc.vector.scalar_tensor_tensor(coef[:, 1, :], u[:], 2.0, rz, ALU.mult, ALU.mult)
+        nc.gpsimd.tensor_tensor(by_group(sn[:]), by_group(p), spread(an[:]), ALU.mult)
+        for h in range(HALVES):
+            nc.vector.tensor_tensor(by_group(dev[:, cols[h]]), by_group(a_ps[h][:]), spread(mean[:, groups[h]]), ALU.subtract)
+        for h in range(HALVES):
+            nc.vector.tensor_tensor(w_a[:, cols[h]], t_ps[h][:, 0, :], dev[:, cols[h]], ALU.mult)
+        for h in range(HALVES):
+            nc.vector.tensor_tensor(w_b[:, cols[h]], t_ps[h][:, 1, :], w_a[:, cols[h]], ALU.add)
+        for h in range(HALVES):
+            nc.vector.tensor_tensor(wt[:, 0, cols[h]], w_b[:, cols[h]], sn[:, cols[h]], ALU.mult)
+        for h in range(HALVES):
+            nc.vector.tensor_tensor(wt[:, 1, cols[h]], t_ps[h][:, 0, :], sn[:, cols[h]], ALU.mult)
+        nc.gpsimd.tensor_tensor(rest[:], base_sb[:], wt[:, 0, :], ALU.subtract)
+        for h in range(HALVES):
+            group_sums(xs, wt, h)
+        for h in range(HALVES):
+            g = groups[h]
+            nc.vector.tensor_tensor(xc[:, :, g], xs[:, 0:1, g].to_broadcast([P, 2, GH]), coef[:, :, g], ALU.mult)
+            nc.vector.tensor_tensor(t2[:, g], xs[:, 1, g], rz[:, g], ALU.mult)
+        for h in range(HALVES):
+            g = groups[h]
+            nc.vector.tensor_tensor(cc[:, g], xc[:, 1, g], t2[:, g], ALU.add)
+        for h in range(HALVES):
+            nc.vector.tensor_tensor(by_group(e1[:, cols[h]]), by_group(dev[:, cols[h]]), spread(cc[:, groups[h]]), ALU.mult)
+        for h in range(HALVES):
+            nc.vector.tensor_tensor(by_group(e2[:, cols[h]]), by_group(e1[:, cols[h]]), spread(xc[:, 0, groups[h]]), ALU.add)
+        for h in range(HALVES):
+            nc.vector.tensor_tensor(e3[:, cols[h]], e2[:, cols[h]], p[:, cols[h]], ALU.mult)
+        for h in range(HALVES):
+            nc.vector.tensor_tensor(y[:, cols[h]], e3[:, cols[h]], rest[:, cols[h]], ALU.add)
+            nc.sync.dma_start(out=out[:, cols[h]], in_=y[:, cols[h]])

@@ -41,8 +41,8 @@ def tile_attend_hvgatepool_kernel(tc, tab_words, tab_scales, w1, w2, wo, dy, dta
             return window
 
         def load_scales(window, scales, queue):
-            for q in range(4):
-                queue.dma_start(out=window[32 * q : 32 * q + 4, :].bitcast(I32), in_=scales[0, 4 * q : 4 * q + 4, :].bitcast(I32))
+            for x in range(4):
+                queue.dma_start(out=window[x : P : 32, :].bitcast(I32), in_=scales[0, x : 16 : 4, :].bitcast(I32))
 
         def load_rows(rows, name):
             raw = sb.tile([P, PACK, rows.shape[1]], F32, name=name)
@@ -85,7 +85,7 @@ def tile_attend_hvgatepool_kernel(tc, tab_words, tab_scales, w1, w2, wo, dy, dta
         dy_raw = load_rows(dy, "dy_raw")
         dtab_window = load_words(dtab_words, "dtab_window")
         gain = sb.tile([P, 1], F32, name="gain")
-        nc.sync.dma_start(out=gain[:], in_=og)
+        nc.gpsimd.dma_start(out=gain[:], in_=og)
         base_sb = sb.tile([P, J], F32, name="base_sb")
         nc.sync.dma_start(out=base_sb[:], in_=base)
 
@@ -102,94 +102,96 @@ def tile_attend_hvgatepool_kernel(tc, tab_words, tab_scales, w1, w2, wo, dy, dta
         groups = [slice(h * GH, (h + 1) * GH) for h in range(HALVES)]
         lists = [offsets[:, h * JH // 16 : (h + 1) * JH // 16] for h in range(HALVES)]
 
-        a_ps = [ps.tile([P, JH], F32, name="a_ps%d" % h) for h in range(HALVES)]
+        a_ps = ps.tile([P, J], F32, name="a_ps")
         b_ps = [ps.tile([P, JH], F32, name="b_ps%d" % h) for h in range(HALVES)]
-        t_ps = [ps.tile([P, 2, JH], F32, name="t_ps%d" % h) for h in range(HALVES)]
+        tb_ps = [ps.tile([P, JH], F32, name="tb_ps%d" % h) for h in range(HALVES)]
+        ta_ps = [ps.tile([P, JH], F32, name="ta_ps%d" % h) for h in range(HALVES)]
         c_ps = ps.tile([P, G], F32, name="c_ps")
 
-        p_pa = sb.tile([P, 2, J], F32, name="p_pa")
-        z_n = sb.tile([P, 2, G], F32, name="z_n")
-        coef = sb.tile([P, 2, G], F32, name="coef")
+        p = sb.tile([P, J], F32, name="p")
+        pa = sb.tile([P, J], F32, name="pa")
+        z = sb.tile([P, G], F32, name="z")
+        n1 = sb.tile([P, G], F32, name="n1")
+        cf = sb.tile([P, 3, G], F32, name="cf")
+        rz, ur = cf[:, 0, :], cf[:, 2, :]
+        an_u = sb.tile([P, 2, G], F32, name="an_u")
+        an, u = an_u[:, 0, :], an_u[:, 1, :]
+        um1 = sb.tile([P, G], F32, name="um1")
+        cg = sb.tile([P, G], F32, name="cg")
+        a_sb = sb.tile([P, J], F32, name="a_sb")
+        dev = sb.tile([P, J], F32, name="dev")
         mean = sb.tile([P, G], F32, name="mean")
-        u = sb.tile([P, G], F32, name="u")
         usq = sb.tile([P, G], F32, name="usq")
         a0 = sb.tile([P, G], F32, name="a0")
-        an = sb.tile([P, G], F32, name="an")
-        dev = sb.tile([P, J], F32, name="dev")
         sn = sb.tile([P, J], F32, name="sn")
         w_a = sb.tile([P, J], F32, name="w_a")
         w_b = sb.tile([P, J], F32, name="w_b")
         wt = sb.tile([P, 2, J], F32, name="wt")
         xs = sb.tile([P, 2, G], F32, name="xs")
         xc = sb.tile([P, 2, G], F32, name="xc")
-        t2 = sb.tile([P, G], F32, name="t2")
+        t1 = sb.tile([P, G], F32, name="t1")
         cc = sb.tile([P, G], F32, name="cc")
         e1 = sb.tile([P, J], F32, name="e1")
         e2 = sb.tile([P, J], F32, name="e2")
         e3 = sb.tile([P, J], F32, name="e3")
         rest = sb.tile([P, J], F32, name="rest")
         y = sb.tile([P, J], F32, name="y")
-        p = p_pa[:, 0, :]
-        rz = coef[:, 0, :]
 
-        def group_sums(sums, terms, h):
-            nc.vector.tensor_reduce(sums[:, :, groups[h]], terms[:, :, cols[h]].rearrange("p k (g i) -> p k g i", i=POOL), AX.X, ALU.add)
-
-        def gather_directions(h):
-            dtab_w = sb.tile([P, JH], U32, name="dtab_w%d" % h, align_bytes=64)
-            nc.vector.tensor_copy(dtab_w[:], dtab_window[:].indirect(lists[h]))
-            product(t_ps[h][:, 0, :], w2_q, dtab_w[:], dtab_s[:, cols[h]])
-            product(t_ps[h][:, 1, :], w1_q, dtab_w[:], dtab_s[:, cols[h]])
-
-        tab_w = [sb.tile([P, JH], U32, name="tab_w%d" % h, align_bytes=64) for h in range(HALVES)]
+        tab_w = sb.tile([P, J], U32, name="tab_w", align_bytes=64)
         for h in range(HALVES):
-            nc.vector.tensor_copy(tab_w[h][:], tab_window[:].indirect(lists[h]))
-            product(b_ps[h][:], w2_q, tab_w[h][:], tab_s[:, cols[h]])
+            nc.vector.tensor_copy(tab_w[:, cols[h]], tab_window[:].indirect(lists[h]))
+            product(b_ps[h][:], w2_q, tab_w[:, cols[h]], tab_s[:, cols[h]])
         w1_q = cast_and_quantize(w1_raw, "w1")
+        product(a_ps[:], w1_q, tab_w[:], tab_s[:])
         for h in range(HALVES):
             nc.scalar.activation(p[:, cols[h]], b_ps[h][:], ACT.Exp)
-            product(a_ps[h][:], w1_q, tab_w[h][:], tab_s[:, cols[h]])
         dtab_s = sb.tile([P, J], U8, name="dtab_s", align_bytes=64)
         nc.vector.tensor_copy(dtab_s[:], dtab_scale_window[:].indirect(offsets[:]))
-        for h in range(HALVES):
-            nc.vector.tensor_tensor(p_pa[:, 1, cols[h]], a_ps[h][:], p[:, cols[h]], ALU.mult)
-        for h in range(HALVES):
-            group_sums(z_n, p_pa, h)
 
         wo_q = cast_and_quantize(wo_raw, "wo")
         dy_q = cast_and_quantize(dy_raw, "dy")
         product(c_ps[:], wo_q, dy_q[0], dy_q[1])
 
-        nc.vector.reciprocal(rz, z_n[:, 0, :])
-        gather_directions(0)
-        nc.vector.tensor_tensor(mean[:], z_n[:, 1, :], rz, ALU.mult)
-        nc.vector.scalar_tensor_tensor(a0[:], c_ps[:], gain[:], rz, ALU.mult, ALU.mult)
-        nc.scalar.activation(u[:], mean[:], ACT.Tanh)
-        nc.scalar.activation(usq[:], u[:], ACT.Square)
-        gather_directions(1)
-        nc.vector.scalar_tensor_tensor(an[:], usq[:], -1.0, a0[:], ALU.add, ALU.mult)
-        nc.vector.scalar_tensor_tensor(coef[:, 1, :], u[:], 2.0, rz, ALU.mult, ALU.mult)
-        nc.gpsimd.tensor_tensor(by_group(sn[:]), by_group(p), spread(an[:]), ALU.mult)
+        nc.vector.tensor_reduce(z[:], by_group(p[:]), AX.X, ALU.add)
+        nc.vector.tensor_tensor(pa[:], a_ps[:], p[:], ALU.mult)
+        nc.scalar.activation(cg[:], c_ps[:], ACT.Copy, scale=gain[:])
+        nc.scalar.copy(a_sb[:], a_ps[:])
+        nc.vector.reciprocal(rz, z[:])
+        nc.vector.tensor_reduce(n1[:], by_group(pa[:]), AX.X, ALU.add)
+        nc.gpsimd.tensor_tensor(a0[:], cg[:], rz, ALU.mult)
+        nc.vector.tensor_tensor(mean[:], n1[:], rz, ALU.mult)
+        nc.scalar.activation(u, mean[:], ACT.Tanh)
+        nc.scalar.activation(usq[:], u, ACT.Square)
+        nc.scalar.activation(um1[:], usq[:], ACT.Copy, bias=-1.0)
+        nc.gpsimd.tensor_tensor(by_group(dev[:]), by_group(a_sb[:]), spread(mean[:]), ALU.subtract)
+        nc.gpsimd.tensor_tensor(an, um1[:], a0[:], ALU.mult)
+        nc.gpsimd.tensor_tensor(by_group(sn[:]), by_group(p[:]), spread(an), ALU.mult)
+        nc.gpsimd.tensor_tensor(cf[:, 1:3, :], an_u[:], rz.unsqueeze(1).to_broadcast([P, 2, G]), ALU.mult)
+
+        dtab_w = sb.tile([P, J], U32, name="dtab_w", align_bytes=64)
         for h in range(HALVES):
-            nc.vector.tensor_tensor(by_group(dev[:, cols[h]]), by_group(a_ps[h][:]), spread(mean[:, groups[h]]), ALU.subtract)
+            nc.vector.tensor_copy(dtab_w[:, cols[h]], dtab_window[:].indirect(lists[h]))
+            product(tb_ps[h][:], w2_q, dtab_w[:, cols[h]], dtab_s[:, cols[h]])
+            product(ta_ps[h][:], w1_q, dtab_w[:, cols[h]], dtab_s[:, cols[h]])
+
         for h in range(HALVES):
-            nc.vector.tensor_tensor(w_a[:, cols[h]], t_ps[h][:, 0, :], dev[:, cols[h]], ALU.mult)
+            nc.vector.tensor_tensor(w_a[:, cols[h]], tb_ps[h][:], dev[:, cols[h]], ALU.mult)
         for h in range(HALVES):
-            nc.vector.tensor_tensor(w_b[:, cols[h]], t_ps[h][:, 1, :], w_a[:, cols[h]], ALU.add)
+            nc.vector.tensor_tensor(w_b[:, cols[h]], ta_ps[h][:], w_a[:, cols[h]], ALU.add)
         for h in range(HALVES):
             nc.vector.tensor_tensor(wt[:, 0, cols[h]], w_b[:, cols[h]], sn[:, cols[h]], ALU.mult)
         for h in range(HALVES):
-            nc.vector.tensor_tensor(wt[:, 1, cols[h]], t_ps[h][:, 0, :], sn[:, cols[h]], ALU.mult)
+            nc.vector.tensor_tensor(wt[:, 1, cols[h]], tb_ps[h][:], p[:, cols[h]], ALU.mult)
         nc.gpsimd.tensor_tensor(rest[:], base_sb[:], wt[:, 0, :], ALU.subtract)
         for h in range(HALVES):
-            group_sums(xs, wt, h)
+            nc.vector.tensor_reduce(xs[:, :, groups[h]], wt[:, :, cols[h]].rearrange("p k (g i) -> p k g i", i=POOL), AX.X, ALU.add)
         for h in range(HALVES):
             g = groups[h]
-            nc.vector.tensor_tensor(xc[:, :, g], xs[:, 0:1, g].to_broadcast([P, 2, GH]), coef[:, :, g], ALU.mult)
-            nc.vector.tensor_tensor(t2[:, g], xs[:, 1, g], rz[:, g], ALU.mult)
+            nc.vector.tensor_tensor(xc[:, :, g], xs[:, :, g], cf[:, 0:2, g], ALU.mult)
+            nc.vector.tensor_tensor(t1[:, g], xs[:, 0, g], ur[:, g], ALU.mult)
         for h in range(HALVES):
             g = groups[h]
-            nc.vector.tensor_tensor(cc[:, g], xc[:, 1, g], t2[:, g], ALU.add)
+            nc.vector.scalar_tensor_tensor(cc[:, g], t1[:, g], 2.0, xc[:, 1, g], ALU.mult, ALU.add)
         for h in range(HALVES):
             nc.vector.tensor_tensor(by_group(e1[:, cols[h]]), by_group(dev[:, cols[h]]), spread(cc[:, groups[h]]), ALU.mult)
         for h in range(HALVES):

@@ -108,29 +108,29 @@ def tile_attend_hvgatepool_kernel(tc, tab_words, tab_scales, w1, w2, wo, dy, dta
         ta_ps = [ps.tile([P, JH], F32, name="ta_ps%d" % h) for h in range(HALVES)]
         c_ps = ps.tile([P, G], F32, name="c_ps")
 
-        p = sb.tile([P, J], F32, name="p")
+        dev_p = sb.tile([P, 2, J], F32, name="dev_p")
+        dev, p = dev_p[:, 0, :], dev_p[:, 1, :]
         pa = sb.tile([P, J], F32, name="pa")
         z = sb.tile([P, G], F32, name="z")
         n1 = sb.tile([P, G], F32, name="n1")
-        cf = sb.tile([P, 3, G], F32, name="cf")
-        rz, ur = cf[:, 0, :], cf[:, 2, :]
-        an_u = sb.tile([P, 2, G], F32, name="an_u")
-        an, u = an_u[:, 0, :], an_u[:, 1, :]
+        cf = sb.tile([P, 2, 2, G], F32, name="cf")
+        rz = cf[:, 1, 1, :]
+        nc.gpsimd.memset(cf[:, 1, 0, :], 0.0)
+        u = sb.tile([P, G], F32, name="u")
+        an_u2 = sb.tile([P, 2, G], F32, name="an_u2")
+        an = an_u2[:, 0, :]
         um1 = sb.tile([P, G], F32, name="um1")
         cg = sb.tile([P, G], F32, name="cg")
         a_sb = sb.tile([P, J], F32, name="a_sb")
-        dev = sb.tile([P, J], F32, name="dev")
         mean = sb.tile([P, G], F32, name="mean")
         usq = sb.tile([P, G], F32, name="usq")
         a0 = sb.tile([P, G], F32, name="a0")
         sn = sb.tile([P, J], F32, name="sn")
-        w_a = sb.tile([P, J], F32, name="w_a")
         w_b = sb.tile([P, J], F32, name="w_b")
-        wt = sb.tile([P, 2, J], F32, name="wt")
+        wt = sb.tile([P, 3, J], F32, name="wt")
         xs = sb.tile([P, 2, G], F32, name="xs")
-        xc = sb.tile([P, 2, G], F32, name="xc")
-        t1 = sb.tile([P, G], F32, name="t1")
-        cc = sb.tile([P, G], F32, name="cc")
+        prod = sb.tile([P, 2, 2, G], F32, name="prod")
+        cx = sb.tile([P, 2, G], F32, name="cx")
         e1 = sb.tile([P, J], F32, name="e1")
         e2 = sb.tile([P, J], F32, name="e2")
         e3 = sb.tile([P, J], F32, name="e3")
@@ -152,21 +152,22 @@ def tile_attend_hvgatepool_kernel(tc, tab_words, tab_scales, w1, w2, wo, dy, dta
         dy_q = cast_and_quantize(dy_raw, "dy")
         product(c_ps[:], wo_q, dy_q[0], dy_q[1])
 
-        nc.vector.tensor_reduce(z[:], by_group(p[:]), AX.X, ALU.add)
-        nc.vector.tensor_tensor(pa[:], a_ps[:], p[:], ALU.mult)
+        nc.vector.tensor_reduce(z[:], by_group(p), AX.X, ALU.add)
+        nc.vector.tensor_tensor(pa[:], a_ps[:], p, ALU.mult)
         nc.scalar.activation(cg[:], c_ps[:], ACT.Copy, scale=gain[:])
         nc.scalar.copy(a_sb[:], a_ps[:])
         nc.vector.reciprocal(rz, z[:])
         nc.vector.tensor_reduce(n1[:], by_group(pa[:]), AX.X, ALU.add)
         nc.gpsimd.tensor_tensor(a0[:], cg[:], rz, ALU.mult)
         nc.vector.tensor_tensor(mean[:], n1[:], rz, ALU.mult)
-        nc.scalar.activation(u, mean[:], ACT.Tanh)
-        nc.scalar.activation(usq[:], u, ACT.Square)
+        nc.scalar.activation(u[:], mean[:], ACT.Tanh)
+        nc.scalar.activation(usq[:], u[:], ACT.Square)
         nc.scalar.activation(um1[:], usq[:], ACT.Copy, bias=-1.0)
-        nc.gpsimd.tensor_tensor(by_group(dev[:]), by_group(a_sb[:]), spread(mean[:]), ALU.subtract)
+        nc.scalar.activation(an_u2[:, 1, :], u[:], ACT.Copy, scale=2.0)
+        nc.gpsimd.tensor_tensor(by_group(dev), by_group(a_sb[:]), spread(mean[:]), ALU.subtract)
         nc.gpsimd.tensor_tensor(an, um1[:], a0[:], ALU.mult)
-        nc.gpsimd.tensor_tensor(by_group(sn[:]), by_group(p[:]), spread(an), ALU.mult)
-        nc.gpsimd.tensor_tensor(cf[:, 1:3, :], an_u[:], rz.unsqueeze(1).to_broadcast([P, 2, G]), ALU.mult)
+        nc.gpsimd.tensor_tensor(by_group(sn[:]), by_group(p), spread(an), ALU.mult)
+        nc.gpsimd.tensor_tensor(cf[:, 0, :, :], an_u2[:], rz.unsqueeze(1).to_broadcast([P, 2, G]), ALU.mult)
 
         dtab_w = sb.tile([P, J], U32, name="dtab_w", align_bytes=64)
         for h in range(HALVES):
@@ -175,27 +176,26 @@ def tile_attend_hvgatepool_kernel(tc, tab_words, tab_scales, w1, w2, wo, dy, dta
             product(ta_ps[h][:], w1_q, dtab_w[:, cols[h]], dtab_s[:, cols[h]])
 
         for h in range(HALVES):
-            nc.vector.tensor_tensor(w_a[:, cols[h]], tb_ps[h][:], dev[:, cols[h]], ALU.mult)
+            nc.vector.tensor_tensor(wt[:, 0:2, cols[h]], tb_ps[h][:].unsqueeze(1).to_broadcast([P, 2, JH]), dev_p[:, :, cols[h]], ALU.mult)
         for h in range(HALVES):
-            nc.vector.tensor_tensor(w_b[:, cols[h]], ta_ps[h][:], w_a[:, cols[h]], ALU.add)
+            nc.vector.tensor_tensor(w_b[:, cols[h]], ta_ps[h][:], wt[:, 0, cols[h]], ALU.add)
+        nc.vector.tensor_reduce(xs[:, 0, :], by_group(wt[:, 1, :]), AX.X, ALU.add)
         for h in range(HALVES):
-            nc.vector.tensor_tensor(wt[:, 0, cols[h]], w_b[:, cols[h]], sn[:, cols[h]], ALU.mult)
+            nc.vector.tensor_tensor(wt[:, 2, cols[h]], w_b[:, cols[h]], sn[:, cols[h]], ALU.mult)
         for h in range(HALVES):
-            nc.vector.tensor_tensor(wt[:, 1, cols[h]], tb_ps[h][:], p[:, cols[h]], ALU.mult)
-        nc.gpsimd.tensor_tensor(rest[:], base_sb[:], wt[:, 0, :], ALU.subtract)
-        for h in range(HALVES):
-            nc.vector.tensor_reduce(xs[:, :, groups[h]], wt[:, :, cols[h]].rearrange("p k (g i) -> p k g i", i=POOL), AX.X, ALU.add)
+            nc.vector.tensor_reduce(xs[:, 1, groups[h]], by_group(wt[:, 2, cols[h]]), AX.X, ALU.add)
         for h in range(HALVES):
             g = groups[h]
-            nc.vector.tensor_tensor(xc[:, :, g], xs[:, :, g], cf[:, 0:2, g], ALU.mult)
-            nc.vector.tensor_tensor(t1[:, g], xs[:, 0, g], ur[:, g], ALU.mult)
+            nc.vector.tensor_tensor(prod[:, :, :, g], xs[:, :, g].unsqueeze(1).to_broadcast([P, 2, 2, GH]), cf[:, :, :, g], ALU.mult)
         for h in range(HALVES):
             g = groups[h]
-            nc.vector.scalar_tensor_tensor(cc[:, g], t1[:, g], 2.0, xc[:, 1, g], ALU.mult, ALU.add)
+            nc.vector.tensor_tensor(cx[:, :, g], prod[:, :, 0, g], prod[:, :, 1, g], ALU.add)
         for h in range(HALVES):
-            nc.vector.tensor_tensor(by_group(e1[:, cols[h]]), by_group(dev[:, cols[h]]), spread(cc[:, groups[h]]), ALU.mult)
+            nc.vector.tensor_tensor(by_group(e1[:, cols[h]]), by_group(dev[:, cols[h]]), spread(cx[:, 0, groups[h]]), ALU.mult)
         for h in range(HALVES):
-            nc.vector.tensor_tensor(by_group(e2[:, cols[h]]), by_group(e1[:, cols[h]]), spread(xc[:, 0, groups[h]]), ALU.add)
+            nc.vector.tensor_tensor(rest[:, cols[h]], base_sb[:, cols[h]], wt[:, 2, cols[h]], ALU.subtract)
+        for h in range(HALVES):
+            nc.vector.tensor_tensor(by_group(e2[:, cols[h]]), by_group(e1[:, cols[h]]), spread(cx[:, 1, groups[h]]), ALU.add)
         for h in range(HALVES):
             nc.vector.tensor_tensor(e3[:, cols[h]], e2[:, cols[h]], p[:, cols[h]], ALU.mult)
         for h in range(HALVES):

@@ -164,7 +164,8 @@ def tile_attend_hvgatepool_kernel(tc, tab_words, tab_scales, w1, w2, wo, dy, dta
         nc.scalar.activation(usq[:], u[:], ACT.Square)
         nc.scalar.activation(um1[:], usq[:], ACT.Copy, bias=-1.0)
         nc.scalar.activation(an_u2[:, 1, :], u[:], ACT.Copy, scale=2.0)
-        nc.gpsimd.tensor_tensor(by_group(dev), by_group(a_sb[:]), spread(mean[:]), ALU.subtract)
+        for h in range(HALVES):
+            nc.gpsimd.tensor_tensor(by_group(dev[:, cols[h]]), by_group(a_sb[:, cols[h]]), spread(mean[:, groups[h]]), ALU.subtract)
         nc.gpsimd.tensor_tensor(an, um1[:], a0[:], ALU.mult)
         nc.gpsimd.tensor_tensor(by_group(sn[:]), by_group(p), spread(an), ALU.mult)
         nc.gpsimd.tensor_tensor(cf[:, 0, :, :], an_u2[:], rz.unsqueeze(1).to_broadcast([P, 2, G]), ALU.mult)

from contextlib import ExitStack

import concourse.mybir as mybir

K, R, F, T, J, G = 512, 128, 512, 2048, 512, 64
FLOPS = 2 * K * R * J * 4 + 2 * F * R * G

F32 = mybir.dt.float32
BF16 = mybir.dt.bfloat16
I32 = mybir.dt.int32
U32 = mybir.dt.uint32
U16 = mybir.dt.uint16
U8 = mybir.dt.uint8
FP8X4 = mybir.dt.float8_e4m3fn_x4
ACT = mybir.ActivationFunctionType
ALU = mybir.AluOpType
AX = mybir.AxisListType

P = 128
PACK = 4
POOL = J // G
HALVES = 2
JH = J // HALVES
GH = G // HALVES


def tile_attend_hvgatepool_kernel(tc, tab_words, tab_scales, w1, w2, wo, dy, dtab_words, dtab_scales, og, base, offs, out):
    nc = tc.nc
    with ExitStack() as ctx:
        sb = ctx.enter_context(tc.tile_pool(name="sb", bufs=1))
        ps = ctx.enter_context(tc.psum_pool(name="ps", bufs=1))

        def load_words(words, name):
            window = sb.tile([P, T], U32, name=name)
            nc.sync.dma_start(out=window[:].bitcast(I32), in_=words[0].rearrange("p n t -> p (n t)").bitcast(I32))
            return window

        def zeroed_scale_window(name, engine):
            window = sb.tile([P, T], U8, name=name)
            engine.memset(window[:].bitcast(I32), 0)
            return window

        def load_scales(window, scales, queue):
            for x in range(4):
                queue.dma_start(out=window[x : P : 32, :].bitcast(I32), in_=scales[0, x : 16 : 4, :].bitcast(I32))

        def load_rows(rows, name):
            raw = sb.tile([P, PACK, rows.shape[1]], F32, name=name)
            nc.sync.dma_start(out=raw[:], in_=rows.rearrange("(p t) c -> p t c", t=PACK))
            return raw

        def interleave(grouped, raw):
            nc.scalar.copy(
                out=grouped.rearrange("p (c i t) -> p c t i", i=4, t=PACK),
                in_=raw[:].rearrange("p t (c i) -> p c t i", i=4),
            )

        def quantize(grouped, name):
            width = grouped.shape[1] // PACK
            codes = sb.tile([P, width], U32, name=name + "_codes", align_bytes=64)
            scales = sb.tile([P, width], U8, name=name + "_scales", align_bytes=64)
            nc.vector.quantize_mx(out=codes[:].bitcast(FP8X4), scales=scales[:], in_=grouped)
            return codes[:], scales[:]

        def product(acc, lhs, rhs_codes, rhs_scales):
            nc.tensor.matmul_mx(out=acc, lhsT=lhs[0].bitcast(FP8X4), lhsT_scale=lhs[1],
                                rhs=rhs_codes.bitcast(FP8X4), rhs_scale=rhs_scales, start=True, stop=True)

        def by_group(ap):
            return ap.rearrange("p (g i) -> p g i", i=POOL)

        def spread(ap):
            return ap.unsqueeze(2).to_broadcast([P, ap.shape[1], POOL])

        offsets = sb.tile([P, J // 16], U16, name="offsets")
        nc.sync.dma_start(offsets[:], offs)
        tab_scale_window = zeroed_scale_window("tab_scale_window", nc.vector)
        dtab_scale_window = zeroed_scale_window("dtab_scale_window", nc.vector)
        w2_raw = load_rows(w2, "w2_raw")
        load_scales(tab_scale_window, tab_scales, nc.sync)
        tab_window = load_words(tab_words, "tab_window")
        w1_raw = load_rows(w1, "w1_raw")
        load_scales(dtab_scale_window, dtab_scales, nc.sync)
        wo_raw = load_rows(wo, "wo_raw")
        dy_raw = load_rows(dy, "dy_raw")
        dtab_window = load_words(dtab_words, "dtab_window")
        gain = sb.tile([P, 1], F32, name="gain")
        nc.gpsimd.dma_start(out=gain[:], in_=og)
        base_sb = sb.tile([P, J], F32, name="base_sb")
        nc.sync.dma_start(out=base_sb[:], in_=base)

        def cast_and_quantize(raw, name):
            grouped = sb.tile([P, raw.shape[2] * PACK], BF16, name=name + "_bf", align_bytes=64)
            interleave(grouped[:], raw)
            return quantize(grouped[:], name)

        tab_s = sb.tile([P, J], U8, name="tab_s", align_bytes=64)
        nc.vector.tensor_copy(tab_s[:], tab_scale_window[:].indirect(offsets[:]))
        w2_q = cast_and_quantize(w2_raw, "w2")

        cols = [slice(h * JH, (h + 1) * JH) for h in range(HALVES)]
        groups = [slice(h * GH, (h + 1) * GH) for h in range(HALVES)]
        lists = [offsets[:, h * JH // 16 : (h + 1) * JH // 16] for h in range(HALVES)]

        a_ps = ps.tile([P, J], F32, name="a_ps")
        b_ps = [ps.tile([P, JH], F32, name="b_ps%d" % h) for h in range(HALVES)]
        tb_ps = [ps.tile([P, JH], F32, name="tb_ps%d" % h) for h in range(HALVES)]
        ta_ps = [ps.tile([P, JH], F32, name="ta_ps%d" % h) for h in range(HALVES)]
        c_ps = ps.tile([P, G], F32, name="c_ps")

        dev_p = sb.tile([P, 2, J], F32, name="dev_p")
        dev, p = dev_p[:, 0, :], dev_p[:, 1, :]
        pa = sb.tile([P, J], F32, name="pa")
        z = sb.tile([P, G], F32, name="z")
        n1 = sb.tile([P, G], F32, name="n1")
        cf = sb.tile([P, 2, 2, G], F32, name="cf")
        rz = cf[:, 1, 1, :]
        nc.gpsimd.memset(cf[:, 1, 0, :], 0.0)
        u = sb.tile([P, G], F32, name="u")
        an_u2 = sb.tile([P, 2, G], F32, name="an_u2")
        an = an_u2[:, 0, :]
        um1 = sb.tile([P, G], F32, name="um1")
        cg = sb.tile([P, G], F32, name="cg")
        a_sb = sb.tile([P, J], F32, name="a_sb")
        mean = sb.tile([P, G], F32, name="mean")
        usq = sb.tile([P, G], F32, name="usq")
        a0 = sb.tile([P, G], F32, name="a0")
        sn = sb.tile([P, J], F32, name="sn")
        w_b = sb.tile([P, J], F32, name="w_b")
        wt = sb.tile([P, 3, J], F32, name="wt")
        xs = sb.tile([P, 2, G], F32, name="xs")
        prod = sb.tile([P, 2, 2, G], F32, name="prod")
        cx = sb.tile([P, 2, G], F32, name="cx")
        e1 = sb.tile([P, J], F32, name="e1")
        e2 = sb.tile([P, J], F32, name="e2")
        e3 = sb.tile([P, J], F32, name="e3")
        rest = sb.tile([P, J], F32, name="rest")
        y = sb.tile([P, J], F32, name="y")

        tab_w = sb.tile([P, J], U32, name="tab_w", align_bytes=64)
        for h in range(HALVES):
            nc.vector.tensor_copy(tab_w[:, cols[h]], tab_window[:].indirect(lists[h]))
            product(b_ps[h][:], w2_q, tab_w[:, cols[h]], tab_s[:, cols[h]])
        w1_q = cast_and_quantize(w1_raw, "w1")
        product(a_ps[:], w1_q, tab_w[:], tab_s[:])
        for h in range(HALVES):
            nc.scalar.activation(p[:, cols[h]], b_ps[h][:], ACT.Exp)
        dtab_s = sb.tile([P, J], U8, name="dtab_s", align_bytes=64)
        nc.vector.tensor_copy(dtab_s[:], dtab_scale_window[:].indirect(offsets[:]))

        wo_q = cast_and_quantize(wo_raw, "wo")
        dy_q = cast_and_quantize(dy_raw, "dy")
        product(c_ps[:], wo_q, dy_q[0], dy_q[1])

        nc.vector.tensor_reduce(z[:], by_group(p), AX.X, ALU.add)
        nc.vector.tensor_tensor(pa[:], a_ps[:], p, ALU.mult)
        nc.scalar.activation(cg[:], c_ps[:], ACT.Copy, scale=gain[:])
        nc.scalar.copy(a_sb[:], a_ps[:])
        nc.vector.reciprocal(rz, z[:])
        nc.vector.tensor_reduce(n1[:], by_group(pa[:]), AX.X, ALU.add)
        nc.gpsimd.tensor_tensor(a0[:], cg[:], rz, ALU.mult)
        nc.vector.tensor_tensor(mean[:], n1[:], rz, ALU.mult)
        nc.scalar.activation(u[:], mean[:], ACT.Tanh)
        nc.scalar.activation(usq[:], u[:], ACT.Square)
        nc.scalar.activation(um1[:], usq[:], ACT.Copy, bias=-1.0)
        nc.scalar.activation(an_u2[:, 1, :], u[:], ACT.Copy, scale=2.0)
        for h in range(HALVES):
            nc.gpsimd.tensor_tensor(by_group(dev[:, cols[h]]), by_group(a_sb[:, cols[h]]), spread(mean[:, groups[h]]), ALU.subtract)
        nc.gpsimd.tensor_tensor(an, um1[:], a0[:], ALU.mult)
        nc.gpsimd.tensor_tensor(by_group(sn[:]), by_group(p), spread(an), ALU.mult)
        nc.gpsimd.tensor_tensor(cf[:, 0, :, :], an_u2[:], rz.unsqueeze(1).to_broadcast([P, 2, G]), ALU.mult)

        dtab_w = sb.tile([P, J], U32, name="dtab_w", align_bytes=64)
        for h in range(HALVES):
            nc.vector.tensor_copy(dtab_w[:, cols[h]], dtab_window[:].indirect(lists[h]))
            product(tb_ps[h][:], w2_q, dtab_w[:, cols[h]], dtab_s[:, cols[h]])
            product(ta_ps[h][:], w1_q, dtab_w[:, cols[h]], dtab_s[:, cols[h]])

        for h in range(HALVES):
            nc.vector.tensor_tensor(wt[:, 0:2, cols[h]], tb_ps[h][:].unsqueeze(1).to_broadcast([P, 2, JH]), dev_p[:, :, cols[h]], ALU.mult)
        for h in range(HALVES):
            nc.vector.tensor_tensor(w_b[:, cols[h]], ta_ps[h][:], wt[:, 0, cols[h]], ALU.add)
        nc.vector.tensor_reduce(xs[:, 0, :], by_group(wt[:, 1, :]), AX.X, ALU.add)
        for h in range(HALVES):
            nc.vector.tensor_tensor(wt[:, 2, cols[h]], w_b[:, cols[h]], sn[:, cols[h]], ALU.mult)
        for h in range(HALVES):
            nc.vector.tensor_reduce(xs[:, 1, groups[h]], by_group(wt[:, 2, cols[h]]), AX.X, ALU.add)
        for h in range(HALVES):
            g = groups[h]
            nc.vector.tensor_tensor(prod[:, :, :, g], xs[:, :, g].unsqueeze(1).to_broadcast([P, 2, 2, GH]), cf[:, :, :, g], ALU.mult)
        for h in range(HALVES):
            g = groups[h]
            nc.vector.tensor_tensor(cx[:, :, g], prod[:, :, 0, g], prod[:, :, 1, g], ALU.add)
        for h in range(HALVES):
            nc.vector.tensor_tensor(by_group(e1[:, cols[h]]), by_group(dev[:, cols[h]]), spread(cx[:, 0, groups[h]]), ALU.mult)
        for h in range(HALVES):
            nc.vector.tensor_tensor(rest[:, cols[h]], base_sb[:, cols[h]], wt[:, 2, cols[h]], ALU.subtract)
        for h in range(HALVES):
            nc.vector.tensor_tensor(by_group(e2[:, cols[h]]), by_group(e1[:, cols[h]]), spread(cx[:, 1, groups[h]]), ALU.add)
        for h in range(HALVES):
            nc.vector.tensor_tensor(e3[:, cols[h]], e2[:, cols[h]], p[:, cols[h]], ALU.mult)
        for h in range(HALVES):
            nc.vector.tensor_tensor(y[:, cols[h]], e3[:, cols[h]], rest[:, cols[h]], ALU.add)
            nc.sync.dma_start(out=out[:, cols[h]], in_=y[:, cols[h]])
